import numpy as np
import ml_dtypes


def mxq(x, axis, fmt="e4m3"):
    dtype, down = {"e4m3": (ml_dtypes.float8_e4m3fn, 7), "e5m2": (ml_dtypes.float8_e5m2, 14)}[fmt]
    v = np.moveaxis(np.asarray(x, np.float32).astype(ml_dtypes.bfloat16).astype(np.float64), axis, -1)
    blocks = v.reshape(v.shape[:-1] + (-1, 32))
    amax = np.abs(blocks).max(-1, keepdims=True)
    byte = np.maximum(np.where(amax > 0, np.frexp(amax)[1] - 1 + 127, 0) - down, 1)
    scale = np.exp2(byte - 127.0)
    codes = (blocks / scale).astype(np.float32).astype(dtype).astype(np.float64)
    return np.moveaxis((codes * scale).reshape(v.shape), -1, axis)


WIDE = False


def mx_kscale(k):
    if not WIDE:
        return np.ones(k)
    levels = np.array([30, -30])
    if k % 512:
        return np.exp2(np.random.permutation(np.resize(levels, k // 32))).repeat(32)
    a = np.empty((k // 512, 16))
    for p in range(k // 512):
        a[p, :8] = np.random.permutation(np.resize(levels, 8))
        for g in range(8):
            far = levels[np.abs(levels - a[p, g]) >= 10]
            a[p, g + 8] = far[np.random.randint(len(far))]
    return np.exp2(a.ravel()).repeat(32)


BF16 = ml_dtypes.bfloat16


def bf(x):
    return np.asarray(x, np.float32).astype(BF16)


def f64(x):
    return np.asarray(x).astype(np.float64)


E2M1 = np.array([0.0, 0.5, 1.0, 1.5, 2.0, 3.0, 4.0, 6.0, -0.0, -0.5, -1.0, -1.5, -2.0, -3.0, -4.0, -6.0])


def pack_weight(w, fmt):
    k, n = w.shape
    w = f64(bf(w)).reshape(k // 32, 32, n)
    amax = np.abs(w).max(1)
    if fmt == "e4m3":
        byte = np.frexp(amax)[1] - 1 + 127 - 7
    else:
        mant, ex = np.frexp(amax / 6.0)
        byte = np.where(mant > 0.5, ex, ex - 1) + 127
    byte = np.clip(np.where(amax > 0, byte, 1), 1, 254)
    scaled = (w * np.exp2(127.0 - byte)[:, None, :]).reshape(k, n).astype(np.float32)
    by_word = np.ascontiguousarray(scaled.reshape(k // 512, 128, 4, n).transpose(0, 1, 3, 2))
    if fmt == "e4m3":
        words = by_word.astype(ml_dtypes.float8_e4m3fn).view(np.uint8)
    else:
        c = by_word.astype(ml_dtypes.float4_e2m1fn).view(np.uint8) & 0xF
        words = c[..., 0::2] | (c[..., 1::2] << 4)
    return np.ascontiguousarray(words), np.ascontiguousarray(byte.astype(np.uint8).reshape(k // 512, 16, n))


def unpack_weight(words, scales, fmt):
    g, p, n, _ = words.shape
    if fmt == "e4m3":
        vals = np.ascontiguousarray(words).view(ml_dtypes.float8_e4m3fn).astype(np.float64)
    else:
        nib = np.empty((g, p, n, 4), np.uint8)
        nib[..., 0::2] = words & 0xF
        nib[..., 1::2] = words >> 4
        vals = E2M1[nib]
    vals = vals * np.repeat(np.exp2(scales.astype(np.float64) - 127.0), 8, axis=1)[..., None]
    return vals.transpose(0, 1, 3, 2).reshape(g * 512, n)
def pack4(w):
    words, scales = pack_weight(w, "e2m1")
    return words.reshape(words.shape[0], 128, -1), scales


def unpack4(words, scales):
    return unpack_weight(words.reshape(words.shape[0], 128, -1, 2), scales, "e2m1")


B, C, D = 1024, 1024, 2048
EPS, SPREAD, BIAS = 0.5, 0.1, 0.3


def setup_inputs():
    s = mx_kscale(C)
    t = mx_kscale(D)
    base = np.random.standard_normal((D, C)) / np.sqrt(D)
    v_words, v_scales = pack4(base.T / s[:, None] * t)
    return {"err": bf(np.random.standard_normal((B, C)) * s),
            "v_words": v_words,
            "v_scales": v_scales,
            "x": bf(np.random.standard_normal((B, D)) * t),
            "eps": bf(EPS * (1 + SPREAD * np.random.uniform(-1, 1, D)) * t),
            "w": bf(base / t[:, None]),
            "b": bf(BIAS * np.random.standard_normal(C))}


def reference(err, v_words, v_scales, x, eps, w, b):
    v = unpack4(v_words, v_scales)
    grad = mxq(f64(err), 1, "e4m3") @ v
    e = f64(eps)
    delta = np.minimum(np.maximum(grad, -e), e)
    adv = f64(x) + delta
    logits = mxq(adv, 1, "e5m2") @ mxq(f64(w), 0, "e4m3")
    return logits + f64(b)

@@ -1,0 +1,394 @@
+from contextlib import ExitStack
+
+import concourse.mybir as mybir
+from concourse.masks import make_identity
+
+B, C, D = 1024, 1024, 2048
+FLOPS = 2 * B * C * D * 2
+
+F32 = mybir.dt.float32
+BF16 = mybir.dt.bfloat16
+I32 = mybir.dt.int32
+U32 = mybir.dt.uint32
+U8 = mybir.dt.uint8
+E4M3 = mybir.dt.float8_e4m3fn_x4
+E5M2 = mybir.dt.float8_e5m2_x4
+E2M1 = mybir.dt.float4_e2m1fn_x4
+ALU = mybir.AluOpType
+
+P = 128
+PACK = 4
+KP = 512
+N = 512
+NG = D // KP
+NH = B // N
+NC = C // N
+NE = C // KP
+NJ = N // P
+BANKS = {"t": 4, "g": 4}
+
+
+def tile_clipped_gradient_adversary_s9_kernel(tc, err, v_words, v_scales, x, eps, w, b, out):
+    nc = tc.nc
+    with ExitStack() as ctx:
+        keep = ctx.enter_context(tc.tile_pool(name="keep", bufs=1))
+        work = ctx.enter_context(tc.tile_pool(name="work", bufs=2))
+        psum = ctx.enter_context(tc.psum_pool(name="psum", bufs=1))
+        ctx.enter_context(tc.manual_schedule())
+
+        raw = {}
+        ident = keep.tile([P, P], F32, name="ident")
+        make_identity(nc, ident[:])
+
+        def load_rows(key, src, r0, nj, c0):
+            t = keep.tile([P, nj * KP], BF16, name="raw_%s_%d_%d_%d" % key)
+            nc.sync.dma_start(
+                out=t[:].rearrange("p (j k) -> p j k", j=nj),
+                in_=src[r0 : r0 + nj * P, c0 : c0 + KP].rearrange("(j p) k -> p j k", p=P),
+            )
+            raw[key] = t
+
+        def load_err(h, g, half):
+            load_rows(("e", h, g, half), err, h * N + half * 2 * P, 2, g * KP)
+
+        def load_x(k, half):
+            h, g = divmod(k, NG)
+            load_rows(("x", h, g, half), x, h * N + half * 2 * P, 2, g * KP)
+
+        def load_w(g, ch):
+            t = keep.tile([P, PACK * N], BF16, name="raw_w_%d_%d" % (g, ch))
+            nc.sync.dma_start(
+                out=t[:].rearrange("p (j n) -> p j n", j=PACK),
+                in_=w[g * KP : (g + 1) * KP, ch * N : (ch + 1) * N].rearrange("(p j) n -> p j n", j=PACK),
+            )
+            raw[("w", g, ch)] = t
+
+        def load_v(g):
+            t = keep.tile([P, NE * 256], I32, name="raw_v_%d" % g)
+            nc.sync.dma_start(
+                out=t[:].rearrange("p (e n) -> p e n", e=NE),
+                in_=v_words.bitcast(I32)[:, :, g * 256 : (g + 1) * 256].rearrange("e p n -> p e n"),
+            )
+            raw[("v", g)] = t
+
+        vs_raw = keep.tile([P, NE * D // 4], I32, name="vs_raw")
+        nc.vector.memset(vs_raw[:], 0)
+
+        def load_v_scales():
+            for r in range(4):
+                nc.sync.dma_start(
+                    out=vs_raw[r:P:32, :].rearrange("q (e n) -> q e n", e=NE),
+                    in_=v_scales.bitcast(I32)[:, r:16:4, :].rearrange("e q n -> q e n"),
+                )
+
+        eps_raw = keep.tile([P, NG * PACK], BF16, name="eps_raw")
+        bias = keep.tile([P, C], BF16, name="bias")
+
+        load_err(0, 0, 0)
+        load_v(0)
+        load_err(0, 0, 1)
+        load_v_scales()
+        load_err(0, 1, 0)
+        load_err(0, 1, 1)
+        load_v(1)
+        load_x(0, 0)
+        load_x(0, 1)
+        nc.sync.dma_start(
+            out=eps_raw[:].rearrange("p (g t) -> p g t", t=PACK),
+            in_=eps.rearrange("(g p t) -> p g t", p=P, t=PACK),
+        )
+        load_v(2)
+        load_x(1, 0)
+        load_x(1, 1)
+        load_v(3)
+        for g in range(NE):
+            load_err(1, g, 0)
+            load_err(1, g, 1)
+        for k in range(2, NH * NG):
+            load_x(k, 0)
+            load_x(k, 1)
+            if k >= NG:
+                load_w(k - NG, 0)
+        for g in range(NG):
+            load_w(g, 1)
+        nc.sync.dma_start(out=bias[:], in_=b.partition_broadcast(P))
+
+        eps_hi = keep.tile([P, NG * PACK], F32, name="eps_hi")
+        eps_lo = keep.tile([P, NG * PACK], F32, name="eps_lo")
+        nc.gpsimd.tensor_scalar(out=eps_hi[:], in0=eps_raw[:], scalar1=1.0, scalar2=0.0, op0=ALU.mult, op1=ALU.add)
+        nc.gpsimd.tensor_scalar(out=eps_lo[:], in0=eps_raw[:], scalar1=-1.0, scalar2=0.0, op0=ALU.mult, op1=ALU.add)
+
+        v_codes, v_plane = {}, {}
+
+        def sort_v_codes(g):
+            t = keep.tile([P, NE * PACK * 256], U8, name="v_codes_%d" % g, align_bytes=64)
+            nc.vector.tensor_copy(
+                out=t[:].rearrange("p (e t m y) -> p e t m y", e=NE, t=PACK, y=2),
+                in_=raw[("v", g)][:].bitcast(U8).rearrange("p (e m t y) -> p e t m y", e=NE, t=PACK, y=2),
+            )
+            v_codes[g] = t
+
+        def sort_v_scales(g):
+            t = keep.tile([P, NE * KP], U8, name="v_plane_%d" % g, align_bytes=64)
+            src = vs_raw[:].bitcast(U8).rearrange("p (e n) -> p e n", e=NE)[:, :, g * KP : (g + 1) * KP]
+            nc.vector.tensor_copy(
+                out=t[:].rearrange("p (e t m) -> p e t m", e=NE, t=PACK),
+                in_=src.rearrange("p e (m t) -> p e t m", t=PACK),
+            )
+            v_plane[g] = t
+
+        turned = {}
+
+        def new_bank(tag):
+            return psum.tile([P, N], F32, name="bank", tag=tag, bufs=BANKS[tag])
+
+        def turn(h, g, half, tag):
+            if half == 0:
+                turned[(h, g)] = work.tile([P, 2 * N], F32, name="turned", tag="turned", bufs=2, align_bytes=64)
+            dst = turned[(h, g)]
+            bank = new_bank(tag)
+            words = raw[("e", h, g, half)][:].bitcast(F32)
+            for j in range(2):
+                for u in range(2):
+                    nc.tensor.transpose(
+                        bank[:, (2 * j + u) * P : (2 * j + u + 1) * P],
+                        words[:, j * 256 + u : (j + 1) * 256 : 2],
+                        ident[:],
+                    )
+            nc.scalar.copy(
+                out=dst[:, half * N : (half + 1) * N].rearrange("p (j r u) -> p j r u", j=2, u=2),
+                in_=bank[:].rearrange("p (j u r) -> p j r u", j=2, u=2),
+            )
+
+        x_bank = {}
+
+        def turn_x(k):
+            h, g = divmod(k, NG)
+            for u in range(2):
+                x_bank[(k, u)] = new_bank("t")
+                for j in range(NJ):
+                    words = raw[("x", h, g, j // 2)][:].bitcast(F32)
+                    nc.tensor.transpose(
+                        x_bank[(k, u)][:, j * P : (j + 1) * P],
+                        words[:, (j % 2) * 256 + u : (j % 2 + 1) * 256 : 2],
+                        ident[:],
+                    )
+
+        codes, planes = {}, {}
+
+        def new_operand(key):
+            codes[key] = keep.tile([P, N], U32, name="codes_%s_%d_%d" % key, align_bytes=64)
+            planes[key] = keep.tile([P, N], U8, name="plane_%s_%d_%d" % key, align_bytes=64)
+
+        def quantize_err(h, g):
+            new_operand(("e", h, g))
+            nc.vector.quantize_mx(
+                out=codes[("e", h, g)][:].bitcast(E4M3),
+                scales=planes[("e", h, g)][:],
+                in_=turned[(h, g)][:].bitcast(BF16),
+            )
+
+        w_grouped = {}
+
+        def group_w(g, ch, half, on_vector):
+            if half == 0:
+                w_grouped[(g, ch)] = work.tile(
+                    [P, PACK * N], BF16, name="w_grouped", tag="w_grouped", bufs=4, align_bytes=64
+                )
+            dst = w_grouped[(g, ch)][:, half * 2 * N : (half + 1) * 2 * N]
+            src = raw[("w", g, ch)][:].rearrange("p (t n) -> p t n", t=PACK)[:, :, half * N // 2 : (half + 1) * N // 2]
+            dst = dst.rearrange("p (c i t) -> p c t i", i=4, t=PACK)
+            src = src.rearrange("p t (c i) -> p c t i", i=4)
+            if on_vector:
+                nc.vector.tensor_copy(out=dst, in_=src)
+            else:
+                nc.scalar.copy(out=dst, in_=src)
+
+        def quantize_w(g, ch):
+            new_operand(("w", g, ch))
+            nc.vector.quantize_mx(
+                out=codes[("w", g, ch)][:].bitcast(E4M3),
+                scales=planes[("w", g, ch)][:],
+                in_=w_grouped[(g, ch)][:],
+            )
+
+        grad = {}
+
+        def first_pass(k, t, e, bank):
+            h, g = divmod(k, NG)
+            s = e * PACK + t
+            nc.tensor.matmul_mx(
+                out=bank[:],
+                lhsT=v_codes[g][:, s * 256 : (s + 1) * 256].bitcast(E2M1),
+                lhsT_scale=v_plane[g][:, s * P : (s + 1) * P],
+                rhs=codes[("e", h, e)][:].bitcast(E4M3),
+                rhs_scale=planes[("e", h, e)][:],
+                start=(e == 0),
+                stop=(e == NE - 1),
+            )
+
+        def clip(engine, k, t, src):
+            s = (k % NG) * PACK + t
+            engine.tensor_scalar(
+                out=grad[k][:, t * N : (t + 1) * N],
+                in0=src,
+                scalar1=eps_hi[:, s : s + 1],
+                scalar2=eps_lo[:, s : s + 1],
+                op0=ALU.min,
+                op1=ALU.max,
+            )
+
+        def clip_aside(k, t, bank):
+            part = grad[k][:, t * N : (t + 1) * N]
+            nc.scalar.copy(out=part, in_=bank[:])
+            clip(nc.gpsimd, k, t, part)
+
+        held = {}
+
+        def first_product(k, hold):
+            grad[k] = work.tile([P, PACK * N], F32, name="grad", tag="grad", bufs=3)
+            if k == 0:
+                banks = [new_bank("g") for t in range(PACK)]
+                for e in range(NE):
+                    for t in range(PACK):
+                        first_pass(k, t, e, banks[t])
+                for t in range(PACK):
+                    clip_aside(k, t, banks[t])
+            else:
+                for t in range(PACK):
+                    bank = new_bank("g")
+                    for e in range(NE):
+                        first_pass(k, t, e, bank)
+                    if t in hold:
+                        held[(k, t)] = bank
+                    else:
+                        clip_aside(k, t, bank)
+
+        def clip_held(k):
+            for t in range(PACK):
+                if (k, t) in held:
+                    clip(nc.vector, k, t, held[(k, t)][:])
+
+        pairs, adv = {}, {}
+
+        def add_x(k, u):
+            if u == 0:
+                pairs[k] = work.tile([P, 2 * N], F32, name="pairs", tag="pairs", bufs=2, align_bytes=64)
+            nc.vector.tensor_tensor(
+                out=pairs[k][:, u * N : (u + 1) * N].bitcast(BF16).rearrange("p (n e) -> p n e", e=2),
+                in0=grad[k][:, 2 * u * N : 2 * (u + 1) * N].rearrange("p (e n) -> p n e", e=2),
+                in1=x_bank[(k, u)][:].bitcast(BF16).rearrange("p (n e) -> p n e", e=2),
+                op=ALU.add,
+            )
+
+        def join_pairs(k, j0, j1, on_vector=False):
+            if j0 == 0:
+                adv[k] = work.tile([P, 2 * N], F32, name="adv", tag="adv", bufs=2, align_bytes=64)
+            dst = adv[k][:, 2 * j0 * P : 2 * j1 * P].rearrange("p (c i u) -> p c u i", i=2, u=2)
+            src = pairs[k][:].rearrange("p (u n) -> p u n", u=2)[:, :, j0 * P : j1 * P]
+            src = src.rearrange("p u (c i) -> p c u i", i=2)
+            if on_vector:
+                nc.vector.tensor_copy(out=dst, in_=src)
+            else:
+                nc.scalar.copy(out=dst, in_=src)
+
+        def quantize_adv(k, j0, j1):
+            h, g = divmod(k, NG)
+            if j0 == 0:
+                new_operand(("a", h, g))
+            nc.vector.quantize_mx(
+                out=codes[("a", h, g)][:, j0 * P : j1 * P].bitcast(E5M2),
+                scales=planes[("a", h, g)][:, j0 * P : j1 * P],
+                in_=adv[k][:, 2 * j0 * P : 2 * j1 * P].bitcast(BF16),
+            )
+
+        acc = {}
+
+        def second_product(h, j, ch, g0, g1, tag):
+            if g0 == 0:
+                acc[(h, j, ch)] = new_bank(tag)
+            for g in range(g0, g1):
+                nc.tensor.matmul_mx(
+                    out=acc[(h, j, ch)][:],
+                    lhsT=codes[("a", h, g)][:, j * P : (j + 1) * P].bitcast(E5M2),
+                    lhsT_scale=planes[("a", h, g)][:, j * P : (j + 1) * P],
+                    rhs=codes[("w", g, ch)][:].bitcast(E4M3),
+                    rhs_scale=planes[("w", g, ch)][:],
+                    start=(g == 0),
+                    stop=(g == NG - 1),
+                )
+
+        def finish(h, j, ch):
+            res = work.tile([P, N], F32, name="res", tag="res", bufs=6)
+            nc.vector.tensor_tensor(out=res[:], in0=acc[(h, j, ch)][:], in1=bias[:, ch * N : (ch + 1) * N], op=ALU.add)
+            r0 = h * N + j * P
+            nc.sync.dma_start(out=out[r0 : r0 + P, ch * N : (ch + 1) * N], in_=res[:])
+
+        sort_v_codes(0)
+        sort_v_scales(0)
+        turn(0, 0, 0, "t")
+        turn(0, 0, 1, "t")
+        quantize_err(0, 0)
+        turn(0, 1, 0, "t")
+        turn(0, 1, 1, "t")
+        sort_v_codes(1)
+        quantize_err(0, 1)
+        sort_v_scales(1)
+        first_product(0, ())
+        turn_x(0)
+        sort_v_codes(2)
+        sort_v_scales(2)
+        sort_v_scales(3)
+
+        last = NH * NG - 1
+        for k in range(NH * NG):
+            if k < last:
+                first_product(k + 1, (3,) if k >= 1 else ())
+                turn_x(k + 1)
+            if k >= 2:
+                group_w((k - 2) // 2, 0, k % 2, False)
+            if k in (4, 6):
+                quantize_w((k - 4) // 2, 0)
+            add_x(k, 0)
+            add_x(k, 1)
+            join_pairs(k, 0, NJ)
+            if k > 0:
+                quantize_adv(k - 1, 0, NJ)
+            clip_held(k + 1)
+            if k in (0, 1):
+                turn(1, k, 0, "g")
+                turn(1, k, 1, "g")
+            if k == 0:
+                sort_v_codes(3)
+            if k in (1, 2):
+                quantize_err(1, k - 1)
+
+        groups = [(h, j) for h in range(NH) for j in range(NJ)]
+        tags = ["g", "g", "g", "g", "t", "t", "t", "t"]
+        quantize_w(2, 0)
+        group_w(3, 0, 0, False)
+        group_w(3, 0, 1, True)
+        quantize_adv(last, 0, NJ)
+        quantize_w(3, 0)
+        for g in range(2):
+            for (h, j), tag in zip(groups[:6], tags):
+                second_product(h, j, 0, g, g + 1, tag)
+        for (h, j), tag in zip(groups[6:], tags[6:]):
+            second_product(h, j, 0, 0, 2, tag)
+        for g in range(NG - 1):
+            group_w(g, 1, 0, False)
+            group_w(g, 1, 1, False)
+            for h, j in groups[4 * g : 4 * (g + 1)]:
+                second_product(h, j, 0, 2, NG, "")
+                finish(h, j, 0)
+            if g == 2:
+                group_w(NG - 1, 1, 0, True)
+                group_w(NG - 1, 1, 1, True)
+            quantize_w(g, 1)
+        quantize_w(NG - 1, 1)
+        for g in range(2):
+            for (h, j), tag in zip(groups, tags):
+                second_product(h, j, 1, g, g + 1, tag)
+        for h, j in groups:
+            second_product(h, j, 1, 2, NG, "")
+            finish(h, j, 1)

@@ -25,7 +25,8 @@ NH = B // N
 NC = C // N
 NE = C // KP
 NJ = N // P
-BANKS = {"t": 4, "g": 4}
+PLAN = "c0 p0 t000 u000 t001 u001 e00 t010 u010 t011 u011 e01 c1 p1 s000 s001 y000 y010 y020 y030 y001 y011 y021 y031 E00 E01 E02 E03 t100 u100 t101 u101 c2 C00 C01 C02 C03 F10 E10 F11 E11 x00 x01 F12 E12 F13 E13 t110 u110 t111 u111 x10 p2 e10 G10 G11 G12 F20 E20 F21 E21 s100 a00 F22 E22 F23 E23 s101 a01 x11 x20 C13 c3 p3 q00 e11 Q0 G20 G21 G22 F30 E30 F31 E31 s200 a10 F32 E32 F33 E33 s201 a11 x21 x30 C23 q10 Q1 G30 G31 G32 F40 E40 F41 E41 s300 a20 F42 E42 F43 E43 a21 x31 x40 m0_0 m0_1 m1_0 m1_1 C33 q20 Q2 v301 G40 G41 G42 F50 E50 F51 E51 s010 a30 m0_2 m1_2 F52 E52 F53 E53 s011 a31 x41 x50 C43 q30 Q3 G50 G51 G52 G53 F60 E60 F61 E61 s110 a40 m0_3 m1_3 F62 E62 F63 E63 m2_0 m2_1 m2_2 m2_3 a41 x51 x60 v111 f0 f1 q01 Q4 G60 G61 G62 G63 F70 E70 F71 E71 s210 a50 m3_0 m3_1 m3_2 m3_3 F72 E72 F73 E73 s211 s310 f2 a51 x61 x70 v311 f3 q11 Q5 m4_0 m4_1 m5_0 m5_1 m8_0 m8_1 m9_0 m9_1 G70 G71 G72 G73 a60 m6_0 m6_1 a61 x71 q21 q31 Q6 m4_2 m4_3 m5_2 m5_3 m6_2 m6_3 m7_0 m7_1 m7_2 m7_3 m8_2 m9_2 f4 a70 f5 m12_0 m12_1 m12_2 m13_0 m13_1 m13_2 h70 f6 m8_3 m9_3 m12_3 m13_3 a71 f7 m10_0 m10_1 m10_2 m11_0 m11_1 m11_2 h71 f8 f9 m10_3 m11_3 m14_0 m14_1 m14_2 m14_3 f12 f13 m15_0 m15_1 m15_2 m15_3 f10 f11 f14 f15"
+LOADS = "e000 v0 e001 s e010 e011 w00 v1 x00 x01 p v2 e100 e101 x10 v3 x11 w10 e110 e111 x20 x21 w20 x30 x31 w30 b x40 x41 w01 x50 x51 w11 w21 w31 x60 x61 x70 x71"
 
 
 def tile_clipped_gradient_adversary_s9_kernel(tc, err, v_words, v_scales, x, eps, w, b, out):
@@ -53,7 +54,13 @@ def tile_clipped_gradient_adversary_s9_kernel(tc, err, v_words, v_scales, x, eps
 
         def load_x(k, half):
             h, g = divmod(k, NG)
-            load_rows(("x", h, g, half), x, h * N + half * 2 * P, 2, g * KP)
+            r0 = h * N + half * 2 * P
+            t = keep.tile([P, 2 * KP], BF16, name="raw_x_%d_%d" % (k, half))
+            nc.sync.dma_start(
+                out=t[:].rearrange("p (i k) -> p i k", i=2),
+                in_=x[r0 : r0 + 2 * P, g * KP : (g + 1) * KP].rearrange("(p i) k -> p i k", i=2),
+            )
+            raw[("x", k, half)] = t
 
         def load_w(g, ch):
             t = keep.tile([P, PACK * N], BF16, name="raw_w_%d_%d" % (g, ch))
@@ -84,34 +91,25 @@ def tile_clipped_gradient_adversary_s9_kernel(tc, err, v_words, v_scales, x, eps
         eps_raw = keep.tile([P, NG * PACK], BF16, name="eps_raw")
         bias = keep.tile([P, C], BF16, name="bias")
 
-        load_err(0, 0, 0)
-        load_v(0)
-        load_err(0, 0, 1)
-        load_v_scales()
-        load_err(0, 1, 0)
-        load_err(0, 1, 1)
-        load_v(1)
-        load_x(0, 0)
-        load_x(0, 1)
-        nc.sync.dma_start(
-            out=eps_raw[:].rearrange("p (g t) -> p g t", t=PACK),
-            in_=eps.rearrange("(g p t) -> p g t", p=P, t=PACK),
-        )
-        load_v(2)
-        load_x(1, 0)
-        load_x(1, 1)
-        load_v(3)
-        for g in range(NE):
-            load_err(1, g, 0)
-            load_err(1, g, 1)
-        for k in range(2, NH * NG):
-            load_x(k, 0)
-            load_x(k, 1)
-            if k >= NG:
-                load_w(k - NG, 0)
-        for g in range(NG):
-            load_w(g, 1)
-        nc.sync.dma_start(out=bias[:], in_=b.partition_broadcast(P))
+        for it in LOADS.split():
+            c, a = it[0], [int(z) for z in it[1:]]
+            if c == "e":
+                load_err(*a)
+            if c == "v":
+                load_v(*a)
+            if c == "s":
+                load_v_scales()
+            if c == "x":
+                load_x(*a)
+            if c == "w":
+                load_w(*a)
+            if c == "b":
+                nc.sync.dma_start(out=bias[:], in_=b.partition_broadcast(P))
+            if c == "p":
+                nc.sync.dma_start(
+                    out=eps_raw[:].rearrange("p (g t) -> p g t", t=PACK),
+                    in_=eps.rearrange("(g p t) -> p g t", p=P, t=PACK),
+                )
 
         eps_hi = keep.tile([P, NG * PACK], F32, name="eps_hi")
         eps_lo = keep.tile([P, NG * PACK], F32, name="eps_lo")
@@ -139,14 +137,23 @@ def tile_clipped_gradient_adversary_s9_kernel(tc, err, v_words, v_scales, x, eps
 
         turned = {}
 
-        def new_bank(tag):
-            return psum.tile([P, N], F32, name="bank", tag=tag, bufs=BANKS[tag])
+        free_banks = list(range(8))
+        bank_of = {}
 
-        def turn(h, g, half, tag):
-            if half == 0:
-                turned[(h, g)] = work.tile([P, 2 * N], F32, name="turned", tag="turned", bufs=2, align_bytes=64)
-            dst = turned[(h, g)]
-            bank = new_bank(tag)
+        def new_bank(key):
+            n = free_banks[0]
+            free_banks.remove(n)
+            bank_of[key] = n
+            return psum.tile([P, N], F32, name="bank", tag="bank_%d" % n, bufs=1)
+
+        def release(key):
+            free_banks.append(bank_of[key])
+
+        e_bank = {}
+
+        def turn(h, g, half):
+            bank = new_bank(("e", h, g, half))
+            e_bank[(h, g, half)] = bank
             words = raw[("e", h, g, half)][:].bitcast(F32)
             for j in range(2):
                 for u in range(2):
@@ -155,22 +162,26 @@ def tile_clipped_gradient_adversary_s9_kernel(tc, err, v_words, v_scales, x, eps
                         words[:, j * 256 + u : (j + 1) * 256 : 2],
                         ident[:],
                     )
+
+        def unload(h, g, half):
+            if half == 0:
+                turned[(h, g)] = work.tile([P, 2 * N], F32, name="turned", tag="turned", bufs=2, align_bytes=64)
             nc.scalar.copy(
-                out=dst[:, half * N : (half + 1) * N].rearrange("p (j r u) -> p j r u", j=2, u=2),
-                in_=bank[:].rearrange("p (j u r) -> p j r u", j=2, u=2),
+                out=turned[(h, g)][:, half * N : (half + 1) * N].rearrange("p (j r u) -> p j r u", j=2, u=2),
+                in_=e_bank[(h, g, half)][:].rearrange("p (j u r) -> p j r u", j=2, u=2),
             )
+            release(("e", h, g, half))
 
         x_bank = {}
 
-        def turn_x(k):
-            h, g = divmod(k, NG)
-            for u in range(2):
-                x_bank[(k, u)] = new_bank("t")
-                for j in range(NJ):
-                    words = raw[("x", h, g, j // 2)][:].bitcast(F32)
+        def turn_x(k, half):
+            x_bank[(k, half)] = new_bank(("x", k, half))
+            words = raw[("x", k, half)][:].bitcast(F32)
+            for i in range(2):
+                for u in range(2):
                     nc.tensor.transpose(
-                        x_bank[(k, u)][:, j * P : (j + 1) * P],
-                        words[:, (j % 2) * 256 + u : (j % 2 + 1) * 256 : 2],
+                        x_bank[(k, half)][:, (2 * i + u) * P : (2 * i + u + 1) * P],
+                        words[:, i * 256 + u : (i + 1) * 256 : 2],
                         ident[:],
                     )
 
@@ -190,15 +201,16 @@ def tile_clipped_gradient_adversary_s9_kernel(tc, err, v_words, v_scales, x, eps
 
         w_grouped = {}
 
-        def group_w(g, ch, half, on_vector):
-            if half == 0:
+        def group_w(g, ch, part, parts, on_vector):
+            if part == 0:
                 w_grouped[(g, ch)] = work.tile(
-                    [P, PACK * N], BF16, name="w_grouped", tag="w_grouped", bufs=4, align_bytes=64
+                    [P, PACK * N], BF16, name="w_grouped", tag="w_grouped", bufs=3, align_bytes=64
                 )
-            dst = w_grouped[(g, ch)][:, half * 2 * N : (half + 1) * 2 * N]
-            src = raw[("w", g, ch)][:].rearrange("p (t n) -> p t n", t=PACK)[:, :, half * N // 2 : (half + 1) * N // 2]
-            dst = dst.rearrange("p (c i t) -> p c t i", i=4, t=PACK)
-            src = src.rearrange("p t (c i) -> p c t i", i=4)
+            n0, n1 = part * N // parts, (part + 1) * N // parts
+            dst = w_grouped[(g, ch)][:, PACK * n0 : PACK * n1]
+            src = raw[("w", g, ch)][:].rearrange("p (u e n) -> p u e n", u=2, e=2)[:, :, :, n0:n1]
+            dst = dst.rearrange("p (c i e u) -> p c e u i", i=4, e=2, u=2)
+            src = src.rearrange("p u e (c i) -> p c e u i", i=4)
             if on_vector:
                 nc.vector.tensor_copy(out=dst, in_=src)
             else:
@@ -227,10 +239,16 @@ def tile_clipped_gradient_adversary_s9_kernel(tc, err, v_words, v_scales, x, eps
                 stop=(e == NE - 1),
             )
 
+        def region(tile, t):
+            r = 2 * (t % 2) + t // 2
+            return tile[:, r * N : (r + 1) * N]
+
         def clip(engine, k, t, src):
+            if k not in delta:
+                delta[k] = work.tile([P, PACK * N], F32, name="delta", tag="ring_%d" % (k % 3), bufs=1, align_bytes=64)
             s = (k % NG) * PACK + t
             engine.tensor_scalar(
-                out=grad[k][:, t * N : (t + 1) * N],
+                out=region(delta[k], t),
                 in0=src,
                 scalar1=eps_hi[:, s : s + 1],
                 scalar2=eps_lo[:, s : s + 1],
@@ -238,59 +256,35 @@ def tile_clipped_gradient_adversary_s9_kernel(tc, err, v_words, v_scales, x, eps
                 op1=ALU.max,
             )
 
-        def clip_aside(k, t, bank):
-            part = grad[k][:, t * N : (t + 1) * N]
-            nc.scalar.copy(out=part, in_=bank[:])
-            clip(nc.gpsimd, k, t, part)
+        g_bank = {}
+        delta = {}
 
-        held = {}
+        def first_product(k, t, e0, e1):
+            if e0 == 0:
+                g_bank[(k, t)] = new_bank(("g", k, t))
+            for e in range(e0, e1):
+                first_pass(k, t, e, g_bank[(k, t)])
 
-        def first_product(k, hold):
-            grad[k] = work.tile([P, PACK * N], F32, name="grad", tag="grad", bufs=3)
-            if k == 0:
-                banks = [new_bank("g") for t in range(PACK)]
-                for e in range(NE):
-                    for t in range(PACK):
-                        first_pass(k, t, e, banks[t])
-                for t in range(PACK):
-                    clip_aside(k, t, banks[t])
-            else:
-                for t in range(PACK):
-                    bank = new_bank("g")
-                    for e in range(NE):
-                        first_pass(k, t, e, bank)
-                    if t in hold:
-                        held[(k, t)] = bank
-                    else:
-                        clip_aside(k, t, bank)
+        def evac(k, t):
+            if t == 0:
+                grad[k] = work.tile([P, PACK * N], F32, name="grad", tag="grad", bufs=2)
+            nc.scalar.copy(out=region(grad[k], t), in_=g_bank[(k, t)][:])
+            release(("g", k, t))
 
-        def clip_held(k):
-            for t in range(PACK):
-                if (k, t) in held:
-                    clip(nc.vector, k, t, held[(k, t)][:])
+        adv = {}
 
-        pairs, adv = {}, {}
-
-        def add_x(k, u):
-            if u == 0:
-                pairs[k] = work.tile([P, 2 * N], F32, name="pairs", tag="pairs", bufs=2, align_bytes=64)
+        def add_x(k, half):
+            if half == 0:
+                adv[k] = work.tile([P, 2 * N], F32, name="adv", tag="ring_%d" % ((k + 2) % 3), bufs=1, align_bytes=64)
             nc.vector.tensor_tensor(
-                out=pairs[k][:, u * N : (u + 1) * N].bitcast(BF16).rearrange("p (n e) -> p n e", e=2),
-                in0=grad[k][:, 2 * u * N : 2 * (u + 1) * N].rearrange("p (e n) -> p n e", e=2),
-                in1=x_bank[(k, u)][:].bitcast(BF16).rearrange("p (n e) -> p n e", e=2),
+                out=adv[k][:, half * N : (half + 1) * N]
+                .bitcast(BF16)
+                .rearrange("p (c i e u) -> p c e u i", i=2, e=2, u=2),
+                in0=delta[k][:].rearrange("p (e u a c i) -> p a c e u i", e=2, u=2, a=2, i=2)[:, half],
+                in1=x_bank[(k, half)][:].bitcast(BF16).rearrange("p (i u c e) -> p c e u i", i=2, u=2, e=2),
                 op=ALU.add,
             )
-
-        def join_pairs(k, j0, j1, on_vector=False):
-            if j0 == 0:
-                adv[k] = work.tile([P, 2 * N], F32, name="adv", tag="adv", bufs=2, align_bytes=64)
-            dst = adv[k][:, 2 * j0 * P : 2 * j1 * P].rearrange("p (c i u) -> p c u i", i=2, u=2)
-            src = pairs[k][:].rearrange("p (u n) -> p u n", u=2)[:, :, j0 * P : j1 * P]
-            src = src.rearrange("p u (c i) -> p c u i", i=2)
-            if on_vector:
-                nc.vector.tensor_copy(out=dst, in_=src)
-            else:
-                nc.scalar.copy(out=dst, in_=src)
+            release(("x", k, half))
 
         def quantize_adv(k, j0, j1):
             h, g = divmod(k, NG)
@@ -304,9 +298,9 @@ def tile_clipped_gradient_adversary_s9_kernel(tc, err, v_words, v_scales, x, eps
 
         acc = {}
 
-        def second_product(h, j, ch, g0, g1, tag):
+        def second_product(h, j, ch, g0, g1):
             if g0 == 0:
-                acc[(h, j, ch)] = new_bank(tag)
+                acc[(h, j, ch)] = new_bank(("a", h, j, ch))
             for g in range(g0, g1):
                 nc.tensor.matmul_mx(
                     out=acc[(h, j, ch)][:],
@@ -321,74 +315,49 @@ def tile_clipped_gradient_adversary_s9_kernel(tc, err, v_words, v_scales, x, eps
         def finish(h, j, ch):
             res = work.tile([P, N], F32, name="res", tag="res", bufs=6)
             nc.vector.tensor_tensor(out=res[:], in0=acc[(h, j, ch)][:], in1=bias[:, ch * N : (ch + 1) * N], op=ALU.add)
+            release(("a", h, j, ch))
             r0 = h * N + j * P
             nc.sync.dma_start(out=out[r0 : r0 + P, ch * N : (ch + 1) * N], in_=res[:])
 
-        sort_v_codes(0)
-        sort_v_scales(0)
-        turn(0, 0, 0, "t")
-        turn(0, 0, 1, "t")
-        quantize_err(0, 0)
-        turn(0, 1, 0, "t")
-        turn(0, 1, 1, "t")
-        sort_v_codes(1)
-        quantize_err(0, 1)
-        sort_v_scales(1)
-        first_product(0, ())
-        turn_x(0)
-        sort_v_codes(2)
-        sort_v_scales(2)
-        sort_v_scales(3)
-
-        last = NH * NG - 1
-        for k in range(NH * NG):
-            if k < last:
-                first_product(k + 1, (3,) if k >= 1 else ())
-                turn_x(k + 1)
-            if k >= 2:
-                group_w((k - 2) // 2, 0, k % 2, False)
-            if k in (4, 6):
-                quantize_w((k - 4) // 2, 0)
-            add_x(k, 0)
-            add_x(k, 1)
-            join_pairs(k, 0, NJ)
-            if k > 0:
-                quantize_adv(k - 1, 0, NJ)
-            clip_held(k + 1)
-            if k in (0, 1):
-                turn(1, k, 0, "g")
-                turn(1, k, 1, "g")
-            if k == 0:
-                sort_v_codes(3)
-            if k in (1, 2):
-                quantize_err(1, k - 1)
-
-        groups = [(h, j) for h in range(NH) for j in range(NJ)]
-        tags = ["g", "g", "g", "g", "t", "t", "t", "t"]
-        quantize_w(2, 0)
-        group_w(3, 0, 0, False)
-        group_w(3, 0, 1, True)
-        quantize_adv(last, 0, NJ)
-        quantize_w(3, 0)
-        for g in range(2):
-            for (h, j), tag in zip(groups[:6], tags):
-                second_product(h, j, 0, g, g + 1, tag)
-        for (h, j), tag in zip(groups[6:], tags[6:]):
-            second_product(h, j, 0, 0, 2, tag)
-        for g in range(NG - 1):
-            group_w(g, 1, 0, False)
-            group_w(g, 1, 1, False)
-            for h, j in groups[4 * g : 4 * (g + 1)]:
-                second_product(h, j, 0, 2, NG, "")
-                finish(h, j, 0)
-            if g == 2:
-                group_w(NG - 1, 1, 0, True)
-                group_w(NG - 1, 1, 1, True)
-            quantize_w(g, 1)
-        quantize_w(NG - 1, 1)
-        for g in range(2):
-            for (h, j), tag in zip(groups, tags):
-                second_product(h, j, 1, g, g + 1, tag)
-        for h, j in groups:
-            second_product(h, j, 1, 2, NG, "")
-            finish(h, j, 1)
+        groups = [(h, j, ch) for h in range(NH) for ch in range(NC) for j in range(NJ)]
+        for it in PLAN.split():
+            c = it[0]
+            a = [int(z) for z in (it[1:].split("_") if c in "mf" else it[1:])]
+            if c == "s":
+                group_w(a[0], a[1], a[2], 2, False)
+            if c == "v":
+                group_w(a[0], a[1], a[2], 2, True)
+            if c == "q":
+                quantize_w(a[0], a[1])
+            if c == "e":
+                quantize_err(a[0], a[1])
+            if c == "t":
+                turn(a[0], a[1], a[2])
+            if c == "u":
+                unload(a[0], a[1], a[2])
+            if c == "c":
+                sort_v_codes(a[0])
+            if c == "p":
+                sort_v_scales(a[0])
+            if c == "m":
+                second_product(*groups[a[0]], a[1], a[1] + 1)
+            if c == "f":
+                finish(*groups[a[0]])
+            if c == "x":
+                turn_x(a[0], a[1])
+            if c == "y":
+                first_product(a[0], a[1], a[2], a[2] + 1)
+            if c == "F":
+                first_product(a[0], a[1], 0, NE)
+            if c == "E":
+                evac(a[0], a[1])
+            if c == "G":
+                clip(nc.gpsimd, a[0], a[1], region(grad[a[0]], a[1]))
+            if c == "C":
+                clip(nc.vector, a[0], a[1], region(grad[a[0]], a[1]))
+            if c == "a":
+                add_x(a[0], a[1])
+            if c == "Q":
+                quantize_adv(a[0], 0, NJ)
+            if c == "h":
+                quantize_adv(a[0], 2 * a[1], 2 * a[1] + 2)

@@ -25,8 +25,8 @@ NH = B // N
 NC = C // N
 NE = C // KP
 NJ = N // P
-PLAN = "c0 p0 t000 u000 t001 u001 e00 t010 u010 t011 u011 e01 c1 p1 s000 s001 y000 y010 y020 y030 y001 y011 y021 y031 E00 E01 E02 E03 t100 u100 t101 u101 c2 C00 C01 C02 C03 F10 E10 F11 E11 x00 x01 F12 E12 F13 E13 t110 u110 t111 u111 x10 p2 e10 G10 G11 G12 F20 E20 F21 E21 s100 a00 F22 E22 F23 E23 s101 a01 x11 x20 C13 c3 p3 q00 e11 Q0 G20 G21 G22 F30 E30 F31 E31 s200 a10 F32 E32 F33 E33 s201 a11 x21 x30 C23 q10 Q1 G30 G31 G32 F40 E40 F41 E41 s300 a20 F42 E42 F43 E43 a21 x31 x40 m0_0 m0_1 m1_0 m1_1 C33 q20 Q2 v301 G40 G41 G42 F50 E50 F51 E51 s010 a30 m0_2 m1_2 F52 E52 F53 E53 s011 a31 x41 x50 C43 q30 Q3 G50 G51 G52 G53 F60 E60 F61 E61 s110 a40 m0_3 m1_3 F62 E62 F63 E63 m2_0 m2_1 m2_2 m2_3 a41 x51 x60 v111 f0 f1 q01 Q4 G60 G61 G62 G63 F70 E70 F71 E71 s210 a50 m3_0 m3_1 m3_2 m3_3 F72 E72 F73 E73 s211 s310 f2 a51 x61 x70 v311 f3 q11 Q5 m4_0 m4_1 m5_0 m5_1 m8_0 m8_1 m9_0 m9_1 G70 G71 G72 G73 a60 m6_0 m6_1 a61 x71 q21 q31 Q6 m4_2 m4_3 m5_2 m5_3 m6_2 m6_3 m7_0 m7_1 m7_2 m7_3 m8_2 m9_2 f4 a70 f5 m12_0 m12_1 m12_2 m13_0 m13_1 m13_2 h70 f6 m8_3 m9_3 m12_3 m13_3 a71 f7 m10_0 m10_1 m10_2 m11_0 m11_1 m11_2 h71 f8 f9 m10_3 m11_3 m14_0 m14_1 m14_2 m14_3 f12 f13 m15_0 m15_1 m15_2 m15_3 f10 f11 f14 f15"
-LOADS = "e000 v0 e001 s e010 e011 w00 v1 x00 x01 p v2 e100 e101 x10 v3 x11 w10 e110 e111 x20 x21 w20 x30 x31 w30 b x40 x41 w01 x50 x51 w11 w21 w31 x60 x61 x70 x71"
+PLAN = "c0 p0 t000 u000 t001 u001 e00 t010 u010 t011 u011 p1 p2 e01 c1 s000 s001 y000 y010 y020 y030 y001 y011 y021 y031 E00 E01 x00 x01 c2 G00 G01 P02 P03 F10 E10 F11 E11 t100 u100 t101 u101 F12 E12 F13 x10 s100 t110 u110 t111 u111 G10 G11 G12 F20 E20 F21 E21 s101 a00 a01 P13 F22 E22 F23 s200 x11 x20 p3 c3 q00 e10 Q0 G20 G21 G22 F30 E30 F31 E31 s201 a10 a11 P23 F32 E32 F33 s300 x21 x30 q10 e11 Q1 G30 G31 G32 F40 E40 F41 E41 s301 a20 a21 P33 F42 E42 F43 s010 x31 x40 m0_0 m0_1 m1_0 m1_1 q20 Q2 G40 G41 G42 F50 E50 F51 E51 s011 a30 a31 P43 m0_2 m1_2 F52 E52 s110 x41 x50 q30 Q3 G50 G51 G52 m0_3 m1_3 F53 E53 F60 E60 F61 E61 s111 a40 a41 f0 f1 F62 E62 F63 E63 s210 x51 x60 m2_0 m2_1 m2_2 m2_3 m3_0 m3_1 m3_2 m3_3 C53 q01 Q4 q11 G60 G61 G62 s211 s310 s311 a50 m4_0 m4_1 m5_0 m5_1 a51 f2 f3 x61 x70 F70 E70 F71 E71 C63 q21 Q5 q31 m4_2 m4_3 m5_2 m5_3 F72 E72 F73 E73 m6_0 m6_1 m6_2 m6_3 G70 G71 G72 a60 f4 f5 m7_0 m7_1 m7_2 m7_3 a61 x71 m8_0 m8_1 m9_0 m9_1 C73 f6 Q6 m8_2 m9_2 m12_0 m12_1 m12_2 a70 f7 h70 m8_3 m9_3 m12_3 m13_0 m13_1 m13_2 m13_3 a71 f8 h71 m10_0 m10_1 m10_2 m10_3 f9 f12 f13 m11_0 m11_1 m11_2 m11_3 f10 m14_0 m14_1 m14_2 m14_3 f11 m15_0 m15_1 m15_2 m15_3 f14 f15"
+LOADS = "e000 v0 e001 s e010 e011 w00 v1 x00 x01 p v2 e100 e101 x10 w10 e110 e111 v3 x11 x20 w20 x21 x30 w30 x31 x40 w01 x41 x50 w11 b x51 x60 w21 w31 x61 x70 x71"
 
 
 def tile_clipped_gradient_adversary_s9_kernel(tc, err, v_words, v_scales, x, eps, w, b, out):
@@ -266,7 +266,7 @@ def tile_clipped_gradient_adversary_s9_kernel(tc, err, v_words, v_scales, x, eps
                 first_pass(k, t, e, g_bank[(k, t)])
 
         def evac(k, t):
-            if t == 0:
+            if k not in grad:
                 grad[k] = work.tile([P, PACK * N], F32, name="grad", tag="grad", bufs=2)
             nc.scalar.copy(out=region(grad[k], t), in_=g_bank[(k, t)][:])
             release(("g", k, t))
@@ -312,12 +312,19 @@ def tile_clipped_gradient_adversary_s9_kernel(tc, err, v_words, v_scales, x, eps
                     stop=(g == NG - 1),
                 )
 
-        def finish(h, j, ch):
+        def finish(h, j, ch, parts):
             res = work.tile([P, N], F32, name="res", tag="res", bufs=6)
-            nc.vector.tensor_tensor(out=res[:], in0=acc[(h, j, ch)][:], in1=bias[:, ch * N : (ch + 1) * N], op=ALU.add)
-            release(("a", h, j, ch))
             r0 = h * N + j * P
-            nc.sync.dma_start(out=out[r0 : r0 + P, ch * N : (ch + 1) * N], in_=res[:])
+            for part in range(parts):
+                n0, n1 = part * N // parts, (part + 1) * N // parts
+                nc.vector.tensor_tensor(
+                    out=res[:, n0:n1],
+                    in0=acc[(h, j, ch)][:, n0:n1],
+                    in1=bias[:, ch * N + n0 : ch * N + n1],
+                    op=ALU.add,
+                )
+                nc.sync.dma_start(out=out[r0 : r0 + P, ch * N + n0 : ch * N + n1], in_=res[:, n0:n1])
+            release(("a", h, j, ch))
 
         groups = [(h, j, ch) for h in range(NH) for ch in range(NC) for j in range(NJ)]
         for it in PLAN.split():
@@ -342,7 +349,7 @@ def tile_clipped_gradient_adversary_s9_kernel(tc, err, v_words, v_scales, x, eps
             if c == "m":
                 second_product(*groups[a[0]], a[1], a[1] + 1)
             if c == "f":
-                finish(*groups[a[0]])
+                finish(*groups[a[0]], 2 if a[0] == 15 else 1)
             if c == "x":
                 turn_x(a[0], a[1])
             if c == "y":
@@ -355,6 +362,9 @@ def tile_clipped_gradient_adversary_s9_kernel(tc, err, v_words, v_scales, x, eps
                 clip(nc.gpsimd, a[0], a[1], region(grad[a[0]], a[1]))
             if c == "C":
                 clip(nc.vector, a[0], a[1], region(grad[a[0]], a[1]))
+            if c == "P":
+                clip(nc.vector, a[0], a[1], g_bank[(a[0], a[1])][:])
+                release(("g", a[0], a[1]))
             if c == "a":
                 add_x(a[0], a[1])
             if c == "Q":

@@ -25,7 +25,7 @@ NH = B // N
 NC = C // N
 NE = C // KP
 NJ = N // P
-PLAN = "c0 p0 t000 u000 t001 u001 e00 t010 u010 t011 u011 p1 p2 e01 c1 s000 s001 y000 y010 y020 y030 y001 y011 y021 y031 E00 E01 x00 x01 c2 G00 G01 P02 P03 F10 E10 F11 E11 t100 u100 t101 u101 F12 E12 F13 x10 s100 t110 u110 t111 u111 G10 G11 G12 F20 E20 F21 E21 s101 a00 a01 P13 F22 E22 F23 s200 x11 x20 p3 c3 q00 e10 Q0 G20 G21 G22 F30 E30 F31 E31 s201 a10 a11 P23 F32 E32 F33 s300 x21 x30 q10 e11 Q1 G30 G31 G32 F40 E40 F41 E41 s301 a20 a21 P33 F42 E42 F43 s010 x31 x40 m0_0 m0_1 m1_0 m1_1 q20 Q2 G40 G41 G42 F50 E50 F51 E51 s011 a30 a31 P43 m0_2 m1_2 F52 E52 s110 x41 x50 q30 Q3 G50 G51 G52 m0_3 m1_3 F53 E53 F60 E60 F61 E61 s111 a40 a41 f0 f1 F62 E62 F63 E63 s210 x51 x60 m2_0 m2_1 m2_2 m2_3 m3_0 m3_1 m3_2 m3_3 C53 q01 Q4 q11 G60 G61 G62 s211 s310 s311 a50 m4_0 m4_1 m5_0 m5_1 a51 f2 f3 x61 x70 F70 E70 F71 E71 C63 q21 Q5 q31 m4_2 m4_3 m5_2 m5_3 F72 E72 F73 E73 m6_0 m6_1 m6_2 m6_3 G70 G71 G72 a60 f4 f5 m7_0 m7_1 m7_2 m7_3 a61 x71 m8_0 m8_1 m9_0 m9_1 C73 f6 Q6 m8_2 m9_2 m12_0 m12_1 m12_2 a70 f7 h70 m8_3 m9_3 m12_3 m13_0 m13_1 m13_2 m13_3 a71 f8 h71 m10_0 m10_1 m10_2 m10_3 f9 f12 f13 m11_0 m11_1 m11_2 m11_3 f10 m14_0 m14_1 m14_2 m14_3 f11 m15_0 m15_1 m15_2 m15_3 f14 f15"
+PLAN = "c0 p0 t000 u000 t001 u001 e00 t010 u010 t011 u011 p1 p2 e01 c1 s000 s001 y000 y010 y020 y030 y001 y011 y021 y031 E00 E01 x00 x01 c2 G00 G01 P02 P03 F10 E10 F11 E11 t100 u100 t101 u101 F12 E12 F13 x10 s100 t110 u110 t111 u111 G10 G11 G12 F20 E20 F21 E21 s101 a00 a01 P13 F22 E22 F23 s200 x11 x20 p3 c3 q00 e10 e11 Q0 G20 G21 G22 F30 E30 F31 E31 s201 a10 a11 P23 F32 E32 F33 s300 x21 x30 q10 Q1 G30 G31 G32 F40 E40 F41 E41 s301 a20 a21 P33 F42 E42 F43 s010 x31 x40 m0_0 m0_1 m1_0 m1_1 q20 Q2 G40 G41 G42 F50 E50 F51 E51 s011 a30 a31 P43 m0_2 m1_2 F52 E52 s110 x41 x50 q30 Q3 F53 E53 G50 G51 G52 G53 F60 E60 F61 E61 m0_3 m1_3 s111 a40 a41 f0 f1 F62 E62 F63 E63 s210 x51 x60 m2_0 m2_1 m2_2 m2_3 m3_0 m3_1 m3_2 m3_3 q01 q11 Q4 G60 G61 G62 G63 s211 s310 s311 a50 m4_0 m4_1 m5_0 m5_1 a51 f2 f3 x61 x70 x71 F70 E70 F71 E71 q21 Q5 q31 m4_2 m5_2 F72 E72 F73 E73 m4_3 m5_3 m6_0 m6_1 m6_2 m6_3 G70 G71 G72 G73 a60 d4 D4 d5 D5 m7_0 m7_1 m7_2 m7_3 a61 m8_0 m8_1 m9_0 m9_1 d6 D6 Q6 m8_2 m9_2 m12_0 m12_1 m12_2 m13_0 m13_1 m13_2 a70 d7 D7 h70 m8_3 m9_3 m12_3 m13_3 a71 f8 h71 m10_0 m10_1 m10_2 m10_3 f9 f12 f13 m11_0 m11_1 m11_2 m11_3 f10 m14_0 m14_1 m14_2 m14_3 f11 m15_0 m15_1 m15_2 m15_3 f14 f15"
 LOADS = "e000 v0 e001 s e010 e011 w00 v1 x00 x01 p v2 e100 e101 x10 w10 e110 e111 v3 x11 x20 w20 x21 x30 w30 x31 x40 w01 x41 x50 w11 b x51 x60 w21 w31 x61 x70 x71"
 
 
@@ -326,10 +326,23 @@ def tile_clipped_gradient_adversary_s9_kernel(tc, err, v_words, v_scales, x, eps
                 nc.sync.dma_start(out=out[r0 : r0 + P, ch * N + n0 : ch * N + n1], in_=res[:, n0:n1])
             release(("a", h, j, ch))
 
+        sums = {}
+
+        def unload_sum(h, j, ch):
+            sums[(h, j, ch)] = work.tile([P, N], F32, name="res", tag="res", bufs=6)
+            nc.scalar.copy(out=sums[(h, j, ch)][:], in_=acc[(h, j, ch)][:])
+            release(("a", h, j, ch))
+
+        def finish_aside(h, j, ch):
+            res = sums[(h, j, ch)]
+            nc.gpsimd.tensor_tensor(out=res[:], in0=res[:], in1=bias[:, ch * N : (ch + 1) * N], op=ALU.add)
+            r0 = h * N + j * P
+            nc.sync.dma_start(out=out[r0 : r0 + P, ch * N : (ch + 1) * N], in_=res[:])
+
         groups = [(h, j, ch) for h in range(NH) for ch in range(NC) for j in range(NJ)]
         for it in PLAN.split():
             c = it[0]
-            a = [int(z) for z in (it[1:].split("_") if c in "mf" else it[1:])]
+            a = [int(z) for z in (it[1:].split("_") if c in "mfdD" else it[1:])]
             if c == "s":
                 group_w(a[0], a[1], a[2], 2, False)
             if c == "v":
@@ -365,6 +378,10 @@ def tile_clipped_gradient_adversary_s9_kernel(tc, err, v_words, v_scales, x, eps
             if c == "P":
                 clip(nc.vector, a[0], a[1], g_bank[(a[0], a[1])][:])
                 release(("g", a[0], a[1]))
+            if c == "d":
+                unload_sum(*groups[a[0]])
+            if c == "D":
+                finish_aside(*groups[a[0]])
             if c == "a":
                 add_x(a[0], a[1])
             if c == "Q":

from contextlib import ExitStack

import concourse.mybir as mybir
from concourse.masks import make_identity

B, C, D = 1024, 1024, 2048
FLOPS = 2 * B * C * D * 2

F32 = mybir.dt.float32
BF16 = mybir.dt.bfloat16
I32 = mybir.dt.int32
U32 = mybir.dt.uint32
U8 = mybir.dt.uint8
E4M3 = mybir.dt.float8_e4m3fn_x4
E5M2 = mybir.dt.float8_e5m2_x4
E2M1 = mybir.dt.float4_e2m1fn_x4
ALU = mybir.AluOpType

P = 128
PACK = 4
KP = 512
N = 512
NG = D // KP
NH = B // N
NC = C // N
NE = C // KP
NJ = N // P
PLAN = "c0 p0 t000 u000 t001 u001 e00 t010 u010 t011 u011 p1 p2 e01 c1 s000 s001 y000 y010 y020 y030 y001 y011 y021 y031 E00 E01 x00 x01 c2 G00 G01 P02 P03 F10 E10 F11 E11 t100 u100 t101 u101 F12 E12 F13 x10 s100 t110 u110 t111 u111 G10 G11 G12 F20 E20 F21 E21 s101 a00 a01 P13 F22 E22 F23 s200 x11 x20 p3 c3 q00 e10 e11 Q0 G20 G21 G22 F30 E30 F31 E31 s201 a10 a11 P23 F32 E32 F33 s300 x21 x30 q10 Q1 G30 G31 G32 F40 E40 F41 E41 s301 a20 a21 P33 F42 E42 F43 s010 x31 x40 m0_0 m0_1 m1_0 m1_1 q20 Q2 G40 G41 G42 F50 E50 F51 E51 s011 a30 a31 P43 m0_2 m1_2 F52 E52 s110 x41 x50 q30 Q3 F53 E53 G50 G51 G52 G53 F60 E60 F61 E61 m0_3 m1_3 s111 a40 a41 f0 f1 F62 E62 F63 E63 s210 x51 x60 m2_0 m2_1 m2_2 m2_3 m3_0 m3_1 m3_2 m3_3 q01 q11 Q4 G60 G61 G62 G63 s211 s310 s311 a50 m4_0 m4_1 m5_0 m5_1 a51 f2 f3 x61 x70 x71 F70 E70 F71 E71 q21 Q5 q31 m4_2 m5_2 F72 E72 F73 E73 m4_3 m5_3 m6_0 m6_1 m6_2 m6_3 G70 G71 G72 G73 a60 d4 D4 d5 D5 m7_0 m7_1 m7_2 m7_3 a61 m8_0 m8_1 m9_0 m9_1 d6 D6 Q6 m8_2 m9_2 m12_0 m12_1 m12_2 m13_0 m13_1 m13_2 a70 d7 D7 h70 m8_3 m9_3 m12_3 m13_3 a71 f8 h71 m10_0 m10_1 m10_2 m10_3 f9 f12 f13 m11_0 m11_1 m11_2 m11_3 f10 m14_0 m14_1 m14_2 m14_3 f11 m15_0 m15_1 m15_2 m15_3 f14 f15"
LOADS = "e000 v0 e001 s e010 e011 w00 v1 x00 x01 p v2 e100 e101 x10 w10 e110 e111 v3 x11 x20 w20 x21 x30 w30 x31 x40 w01 x41 x50 w11 b x51 x60 w21 w31 x61 x70 x71"


def tile_clipped_gradient_adversary_s9_kernel(tc, err, v_words, v_scales, x, eps, w, b, out):
    nc = tc.nc
    with ExitStack() as ctx:
        keep = ctx.enter_context(tc.tile_pool(name="keep", bufs=1))
        work = ctx.enter_context(tc.tile_pool(name="work", bufs=2))
        psum = ctx.enter_context(tc.psum_pool(name="psum", bufs=1))
        ctx.enter_context(tc.manual_schedule())

        raw = {}
        ident = keep.tile([P, P], F32, name="ident")
        make_identity(nc, ident[:])

        def load_rows(key, src, r0, nj, c0):
            t = keep.tile([P, nj * KP], BF16, name="raw_%s_%d_%d_%d" % key)
            nc.sync.dma_start(
                out=t[:].rearrange("p (j k) -> p j k", j=nj),
                in_=src[r0 : r0 + nj * P, c0 : c0 + KP].rearrange("(j p) k -> p j k", p=P),
            )
            raw[key] = t

        def load_err(h, g, half):
            load_rows(("e", h, g, half), err, h * N + half * 2 * P, 2, g * KP)

        def load_x(k, half):
            h, g = divmod(k, NG)
            r0 = h * N + half * 2 * P
            t = keep.tile([P, 2 * KP], BF16, name="raw_x_%d_%d" % (k, half))
            nc.sync.dma_start(
                out=t[:].rearrange("p (i k) -> p i k", i=2),
                in_=x[r0 : r0 + 2 * P, g * KP : (g + 1) * KP].rearrange("(p i) k -> p i k", i=2),
            )
            raw[("x", k, half)] = t

        def load_w(g, ch):
            t = keep.tile([P, PACK * N], BF16, name="raw_w_%d_%d" % (g, ch))
            nc.sync.dma_start(
                out=t[:].rearrange("p (j n) -> p j n", j=PACK),
                in_=w[g * KP : (g + 1) * KP, ch * N : (ch + 1) * N].rearrange("(p j) n -> p j n", j=PACK),
            )
            raw[("w", g, ch)] = t

        def load_v(g):
            t = keep.tile([P, NE * 256], I32, name="raw_v_%d" % g)
            nc.sync.dma_start(
                out=t[:].rearrange("p (e n) -> p e n", e=NE),
                in_=v_words.bitcast(I32)[:, :, g * 256 : (g + 1) * 256].rearrange("e p n -> p e n"),
            )
            raw[("v", g)] = t

        vs_raw = keep.tile([P, NE * D // 4], I32, name="vs_raw")
        nc.vector.memset(vs_raw[:], 0)

        def load_v_scales():
            for r in range(4):
                nc.sync.dma_start(
                    out=vs_raw[r:P:32, :].rearrange("q (e n) -> q e n", e=NE),
                    in_=v_scales.bitcast(I32)[:, r:16:4, :].rearrange("e q n -> q e n"),
                )

        eps_raw = keep.tile([P, NG * PACK], BF16, name="eps_raw")
        bias = keep.tile([P, C], BF16, name="bias")

        for it in LOADS.split():
            c, a = it[0], [int(z) for z in it[1:]]
            if c == "e":
                load_err(*a)
            if c == "v":
                load_v(*a)
            if c == "s":
                load_v_scales()
            if c == "x":
                load_x(*a)
            if c == "w":
                load_w(*a)
            if c == "b":
                nc.sync.dma_start(out=bias[:], in_=b.partition_broadcast(P))
            if c == "p":
                nc.sync.dma_start(
                    out=eps_raw[:].rearrange("p (g t) -> p g t", t=PACK),
                    in_=eps.rearrange("(g p t) -> p g t", p=P, t=PACK),
                )

        eps_hi = keep.tile([P, NG * PACK], F32, name="eps_hi")
        eps_lo = keep.tile([P, NG * PACK], F32, name="eps_lo")
        nc.gpsimd.tensor_scalar(out=eps_hi[:], in0=eps_raw[:], scalar1=1.0, scalar2=0.0, op0=ALU.mult, op1=ALU.add)
        nc.gpsimd.tensor_scalar(out=eps_lo[:], in0=eps_raw[:], scalar1=-1.0, scalar2=0.0, op0=ALU.mult, op1=ALU.add)

        v_codes, v_plane = {}, {}

        def sort_v_codes(g):
            t = keep.tile([P, NE * PACK * 256], U8, name="v_codes_%d" % g, align_bytes=64)
            nc.vector.tensor_copy(
                out=t[:].rearrange("p (e t m y) -> p e t m y", e=NE, t=PACK, y=2),
                in_=raw[("v", g)][:].bitcast(U8).rearrange("p (e m t y) -> p e t m y", e=NE, t=PACK, y=2),
            )
            v_codes[g] = t

        def sort_v_scales(g):
            t = keep.tile([P, NE * KP], U8, name="v_plane_%d" % g, align_bytes=64)
            src = vs_raw[:].bitcast(U8).rearrange("p (e n) -> p e n", e=NE)[:, :, g * KP : (g + 1) * KP]
            nc.vector.tensor_copy(
                out=t[:].rearrange("p (e t m) -> p e t m", e=NE, t=PACK),
                in_=src.rearrange("p e (m t) -> p e t m", t=PACK),
            )
            v_plane[g] = t

        turned = {}

        free_banks = list(range(8))
        bank_of = {}

        def new_bank(key):
            n = free_banks[0]
            free_banks.remove(n)
            bank_of[key] = n
            return psum.tile([P, N], F32, name="bank", tag="bank_%d" % n, bufs=1)

        def release(key):
            free_banks.append(bank_of[key])

        e_bank = {}

        def turn(h, g, half):
            bank = new_bank(("e", h, g, half))
            e_bank[(h, g, half)] = bank
            words = raw[("e", h, g, half)][:].bitcast(F32)
            for j in range(2):
                for u in range(2):
                    nc.tensor.transpose(
                        bank[:, (2 * j + u) * P : (2 * j + u + 1) * P],
                        words[:, j * 256 + u : (j + 1) * 256 : 2],
                        ident[:],
                    )

        def unload(h, g, half):
            if half == 0:
                turned[(h, g)] = work.tile([P, 2 * N], F32, name="turned", tag="turned", bufs=2, align_bytes=64)
            nc.scalar.copy(
                out=turned[(h, g)][:, half * N : (half + 1) * N].rearrange("p (j r u) -> p j r u", j=2, u=2),
                in_=e_bank[(h, g, half)][:].rearrange("p (j u r) -> p j r u", j=2, u=2),
            )
            release(("e", h, g, half))

        x_bank = {}

        def turn_x(k, half):
            x_bank[(k, half)] = new_bank(("x", k, half))
            words = raw[("x", k, half)][:].bitcast(F32)
            for i in range(2):
                for u in range(2):
                    nc.tensor.transpose(
                        x_bank[(k, half)][:, (2 * i + u) * P : (2 * i + u + 1) * P],
                        words[:, i * 256 + u : (i + 1) * 256 : 2],
                        ident[:],
                    )

        codes, planes = {}, {}

        def new_operand(key):
            codes[key] = keep.tile([P, N], U32, name="codes_%s_%d_%d" % key, align_bytes=64)
            planes[key] = keep.tile([P, N], U8, name="plane_%s_%d_%d" % key, align_bytes=64)

        def quantize_err(h, g):
            new_operand(("e", h, g))
            nc.vector.quantize_mx(
                out=codes[("e", h, g)][:].bitcast(E4M3),
                scales=planes[("e", h, g)][:],
                in_=turned[(h, g)][:].bitcast(BF16),
            )

        w_grouped = {}

        def group_w(g, ch, part, parts, on_vector):
            if part == 0:
                w_grouped[(g, ch)] = work.tile(
                    [P, PACK * N], BF16, name="w_grouped", tag="w_grouped", bufs=3, align_bytes=64
                )
            n0, n1 = part * N // parts, (part + 1) * N // parts
            dst = w_grouped[(g, ch)][:, PACK * n0 : PACK * n1]
            src = raw[("w", g, ch)][:].rearrange("p (u e n) -> p u e n", u=2, e=2)[:, :, :, n0:n1]
            dst = dst.rearrange("p (c i e u) -> p c e u i", i=4, e=2, u=2)
            src = src.rearrange("p u e (c i) -> p c e u i", i=4)
            if on_vector:
                nc.vector.tensor_copy(out=dst, in_=src)
            else:
                nc.scalar.copy(out=dst, in_=src)

        def quantize_w(g, ch):
            new_operand(("w", g, ch))
            nc.vector.quantize_mx(
                out=codes[("w", g, ch)][:].bitcast(E4M3),
                scales=planes[("w", g, ch)][:],
                in_=w_grouped[(g, ch)][:],
            )

        grad = {}

        def first_pass(k, t, e, bank):
            h, g = divmod(k, NG)
            s = e * PACK + t
            nc.tensor.matmul_mx(
                out=bank[:],
                lhsT=v_codes[g][:, s * 256 : (s + 1) * 256].bitcast(E2M1),
                lhsT_scale=v_plane[g][:, s * P : (s + 1) * P],
                rhs=codes[("e", h, e)][:].bitcast(E4M3),
                rhs_scale=planes[("e", h, e)][:],
                start=(e == 0),
                stop=(e == NE - 1),
            )

        def region(tile, t):
            r = 2 * (t % 2) + t // 2
            return tile[:, r * N : (r + 1) * N]

        def clip(engine, k, t, src):
            if k not in delta:
                delta[k] = work.tile([P, PACK * N], F32, name="delta", tag="ring_%d" % (k % 3), bufs=1, align_bytes=64)
            s = (k % NG) * PACK + t
            engine.tensor_scalar(
                out=region(delta[k], t),
                in0=src,
                scalar1=eps_hi[:, s : s + 1],
                scalar2=eps_lo[:, s : s + 1],
                op0=ALU.min,
                op1=ALU.max,
            )

        g_bank = {}
        delta = {}

        def first_product(k, t, e0, e1):
            if e0 == 0:
                g_bank[(k, t)] = new_bank(("g", k, t))
            for e in range(e0, e1):
                first_pass(k, t, e, g_bank[(k, t)])

        def evac(k, t):
            if k not in grad:
                grad[k] = work.tile([P, PACK * N], F32, name="grad", tag="grad", bufs=2)
            nc.scalar.copy(out=region(grad[k], t), in_=g_bank[(k, t)][:])
            release(("g", k, t))

        adv = {}

        def add_x(k, half):
            if half == 0:
                adv[k] = work.tile([P, 2 * N], F32, name="adv", tag="ring_%d" % ((k + 2) % 3), bufs=1, align_bytes=64)
            nc.vector.tensor_tensor(
                out=adv[k][:, half * N : (half + 1) * N]
                .bitcast(BF16)
                .rearrange("p (c i e u) -> p c e u i", i=2, e=2, u=2),
                in0=delta[k][:].rearrange("p (e u a c i) -> p a c e u i", e=2, u=2, a=2, i=2)[:, half],
                in1=x_bank[(k, half)][:].bitcast(BF16).rearrange("p (i u c e) -> p c e u i", i=2, u=2, e=2),
                op=ALU.add,
            )
            release(("x", k, half))

        def quantize_adv(k, j0, j1):
            h, g = divmod(k, NG)
            if j0 == 0:
                new_operand(("a", h, g))
            nc.vector.quantize_mx(
                out=codes[("a", h, g)][:, j0 * P : j1 * P].bitcast(E5M2),
                scales=planes[("a", h, g)][:, j0 * P : j1 * P],
                in_=adv[k][:, 2 * j0 * P : 2 * j1 * P].bitcast(BF16),
            )

        acc = {}

        def second_product(h, j, ch, g0, g1):
            if g0 == 0:
                acc[(h, j, ch)] = new_bank(("a", h, j, ch))
            for g in range(g0, g1):
                nc.tensor.matmul_mx(
                    out=acc[(h, j, ch)][:],
                    lhsT=codes[("a", h, g)][:, j * P : (j + 1) * P].bitcast(E5M2),
                    lhsT_scale=planes[("a", h, g)][:, j * P : (j + 1) * P],
                    rhs=codes[("w", g, ch)][:].bitcast(E4M3),
                    rhs_scale=planes[("w", g, ch)][:],
                    start=(g == 0),
                    stop=(g == NG - 1),
                )

        def finish(h, j, ch, parts):
            res = work.tile([P, N], F32, name="res", tag="res", bufs=6)
            r0 = h * N + j * P
            for part in range(parts):
                n0, n1 = part * N // parts, (part + 1) * N // parts
                nc.vector.tensor_tensor(
                    out=res[:, n0:n1],
                    in0=acc[(h, j, ch)][:, n0:n1],
                    in1=bias[:, ch * N + n0 : ch * N + n1],
                    op=ALU.add,
                )
                nc.sync.dma_start(out=out[r0 : r0 + P, ch * N + n0 : ch * N + n1], in_=res[:, n0:n1])
            release(("a", h, j, ch))

        sums = {}

        def unload_sum(h, j, ch):
            sums[(h, j, ch)] = work.tile([P, N], F32, name="res", tag="res", bufs=6)
            nc.scalar.copy(out=sums[(h, j, ch)][:], in_=acc[(h, j, ch)][:])
            release(("a", h, j, ch))

        def finish_aside(h, j, ch):
            res = sums[(h, j, ch)]
            nc.gpsimd.tensor_tensor(out=res[:], in0=res[:], in1=bias[:, ch * N : (ch + 1) * N], op=ALU.add)
            r0 = h * N + j * P
            nc.sync.dma_start(out=out[r0 : r0 + P, ch * N : (ch + 1) * N], in_=res[:])

        groups = [(h, j, ch) for h in range(NH) for ch in range(NC) for j in range(NJ)]
        for it in PLAN.split():
            c = it[0]
            a = [int(z) for z in (it[1:].split("_") if c in "mfdD" else it[1:])]
            if c == "s":
                group_w(a[0], a[1], a[2], 2, False)
            if c == "v":
                group_w(a[0], a[1], a[2], 2, True)
            if c == "q":
                quantize_w(a[0], a[1])
            if c == "e":
                quantize_err(a[0], a[1])
            if c == "t":
                turn(a[0], a[1], a[2])
            if c == "u":
                unload(a[0], a[1], a[2])
            if c == "c":
                sort_v_codes(a[0])
            if c == "p":
                sort_v_scales(a[0])
            if c == "m":
                second_product(*groups[a[0]], a[1], a[1] + 1)
            if c == "f":
                finish(*groups[a[0]], 2 if a[0] == 15 else 1)
            if c == "x":
                turn_x(a[0], a[1])
            if c == "y":
                first_product(a[0], a[1], a[2], a[2] + 1)
            if c == "F":
                first_product(a[0], a[1], 0, NE)
            if c == "E":
                evac(a[0], a[1])
            if c == "G":
                clip(nc.gpsimd, a[0], a[1], region(grad[a[0]], a[1]))
            if c == "C":
                clip(nc.vector, a[0], a[1], region(grad[a[0]], a[1]))
            if c == "P":
                clip(nc.vector, a[0], a[1], g_bank[(a[0], a[1])][:])
                release(("g", a[0], a[1]))
            if c == "d":
                unload_sum(*groups[a[0]])
            if c == "D":
                finish_aside(*groups[a[0]])
            if c == "a":
                add_x(a[0], a[1])
            if c == "Q":
                quantize_adv(a[0], 0, NJ)
            if c == "h":
                quantize_adv(a[0], 2 * a[1], 2 * a[1] + 2)
